import numpy as np
import ml_dtypes


def mxq(x, axis, fmt="e4m3"):
    dtype, down = {"e4m3": (ml_dtypes.float8_e4m3fn, 7), "e5m2": (ml_dtypes.float8_e5m2, 14)}[fmt]
    v = np.moveaxis(np.asarray(x, np.float32).astype(ml_dtypes.bfloat16).astype(np.float64), axis, -1)
    blocks = v.reshape(v.shape[:-1] + (-1, 32))
    amax = np.abs(blocks).max(-1, keepdims=True)
    byte = np.maximum(np.where(amax > 0, np.frexp(amax)[1] - 1 + 127, 0) - down, 1)
    scale = np.exp2(byte - 127.0)
    codes = (blocks / scale).astype(np.float32).astype(dtype).astype(np.float64)
    return np.moveaxis((codes * scale).reshape(v.shape), -1, axis)


WIDE = False


def mx_kscale(k):
    if not WIDE:
        return np.ones(k)
    levels = np.array([10, -10, 5, -5, 0])
    if k % 512:
        return np.exp2(np.random.permutation(np.resize(levels, k // 32))).repeat(32)
    a = np.empty((k // 512, 16))
    for p in range(k // 512):
        a[p, :8] = np.random.permutation(np.resize(levels, 8))
        for g in range(8):
            far = levels[np.abs(levels - a[p, g]) >= 10]
            a[p, g + 8] = far[np.random.randint(len(far))]
    return np.exp2(a.ravel()).repeat(32)


def f64(x):
    return np.asarray(x).astype(np.float64)


def striped8(idx):
    return np.asarray(idx).reshape(8, -1, 16).transpose(0, 2, 1).reshape(128, -1).astype(np.uint16)


def unstriped8(offs):
    return offs.reshape(8, 16, -1).transpose(0, 2, 1).reshape(8, -1).astype(np.int64)


def pick8(x, idx, run):
    r = np.arange(len(x))
    return x[r[:, None], idx[r % (8 * run) // run]]


E2M1 = np.array([0.0, 0.5, 1.0, 1.5, 2.0, 3.0, 4.0, 6.0, -0.0, -0.5, -1.0, -1.5, -2.0, -3.0, -4.0, -6.0])


def pack_weight(w, fmt):
    k, n = w.shape
    w = f64(np.asarray(w, np.float32).astype(ml_dtypes.bfloat16)).reshape(k // 32, 32, n)
    amax = np.abs(w).max(1)
    if fmt == "e4m3":
        byte = np.frexp(amax)[1] - 1 + 127 - 7
    else:
        mant, ex = np.frexp(amax / 6.0)
        byte = np.where(mant > 0.5, ex, ex - 1) + 127
    byte = np.clip(np.where(amax > 0, byte, 1), 1, 254)
    scaled = (w * np.exp2(127.0 - byte)[:, None, :]).reshape(k, n).astype(np.float32)
    by_word = np.ascontiguousarray(scaled.reshape(k // 512, 128, 4, n).transpose(0, 1, 3, 2))
    if fmt == "e4m3":
        words = by_word.astype(ml_dtypes.float8_e4m3fn).view(np.uint8)
    else:
        c = by_word.astype(ml_dtypes.float4_e2m1fn).view(np.uint8) & 0xF
        words = (c[..., 0::2] | (c[..., 1::2] << 4)).reshape(k // 512, 128, 2 * n)
    return np.ascontiguousarray(words), np.ascontiguousarray(byte.astype(np.uint8).reshape(k // 512, 16, n))


def unpack_weight(words, scales, fmt):
    g, _, n = scales.shape
    words = np.ascontiguousarray(words).reshape(g, 128, n, -1)
    if fmt == "e4m3":
        vals = words.view(ml_dtypes.float8_e4m3fn).astype(np.float64)
    else:
        nib = np.empty((g, 128, n, 4), np.uint8)
        nib[..., 0::2] = words & 0xF
        nib[..., 1::2] = words >> 4
        vals = E2M1[nib]
    vals = vals * np.repeat(np.exp2(scales.astype(np.float64) - 127.0), 8, axis=1)[..., None]
    return vals.transpose(0, 1, 3, 2).reshape(g * 512, n)


def sigmoid(v):
    return 1.0 / (1.0 + np.exp(-v))


D, T, U, X, I, Q = 512, 1024, 1024, 1024, 512, 128


def setup_inputs():
    n = np.random.standard_normal
    idx = np.stack([np.random.permutation(U)[:I] for _ in range(8)])
    idx2 = np.stack([np.random.permutation(T)[:I] for _ in range(8)])
    idx3 = np.stack([np.random.permutation(T)[:I] for _ in range(8)])
    idx4 = np.stack([np.random.permutation(U)[:I] for _ in range(8)])
    idx5 = np.stack([np.random.permutation(X)[:I] for _ in range(8)])
    idx6 = np.stack([np.random.permutation(X)[:I] for _ in range(8)])
    fd = mx_kscale(D)
    cachep = pack_weight(n((D, T)) / fd[:, None], "e4m3")
    draftp = pack_weight(n((D, U)) / fd[:, None], "e2m1")
    archp = pack_weight(n((D, X)) / fd[:, None], "e4m3")
    return {
        "query": (n((D, Q)) * 1.0 / np.sqrt(D) * fd[:, None]).astype(np.float32),
        "cache_words": cachep[0],
        "cache_scales": cachep[1],
        "draft_words": draftp[0],
        "draft_scales": draftp[1],
        "arch_words": archp[0],
        "arch_scales": archp[1],
        "offs": striped8(idx),
        "offs2": striped8(idx2),
        "offs3": striped8(idx3),
        "offs4": striped8(idx4),
        "offs5": striped8(idx5),
        "offs6": striped8(idx6),
    }


def reference(query, cache_words, cache_scales, draft_words, draft_scales, arch_words, arch_scales, offs, offs2, offs3, offs4, offs5, offs6):
    idx = unstriped8(offs)
    idx2 = unstriped8(offs2)
    idx3 = unstriped8(offs3)
    idx4 = unstriped8(offs4)
    idx5 = unstriped8(offs5)
    idx6 = unstriped8(offs6)
    cacheu = unpack_weight(cache_words, cache_scales, "e4m3")
    draftu = unpack_weight(draft_words, draft_scales, "e2m1")
    archu = unpack_weight(arch_words, arch_scales, "e4m3")
    queryq = mxq(f64(query), 0, "e4m3")
    a = queryq.T @ cacheu
    b = queryq.T @ draftu
    c0 = queryq.T @ archu
    f1 = np.zeros((Q, T))
    f1[np.arange(Q)[:, None], idx2[np.arange(Q) % 128 // 16]] = pick8(b, idx, 16)
    sg = sigmoid(f1 * 2.0)
    mg = a * sg
    w = np.maximum(pick8(mg, idx3, 16), pick8(b, idx4, 16))
    f2 = np.zeros((Q, X))
    f2[np.arange(Q)[:, None], idx5[np.arange(Q) % 128 // 16]] = w
    cc = c0 - f2
    y = pick8(cc, idx6, 16) + pick8(mg, idx3, 16)
    return y

@@ -1,0 +1,142 @@
+from contextlib import ExitStack
+
+import concourse.mybir as mybir
+
+D, T, SLOTS, Q = 512, 1024, 512, 128
+FLOPS = 3 * 2 * D * T * Q
+
+F32 = mybir.dt.float32
+BF16 = mybir.dt.bfloat16
+I32 = mybir.dt.int32
+U32 = mybir.dt.uint32
+U16 = mybir.dt.uint16
+U8 = mybir.dt.uint8
+FP8X4 = mybir.dt.float8_e4m3fn_x4
+FP4X4 = mybir.dt.float4_e2m1fn_x4
+ALU = mybir.AluOpType
+ACT = mybir.ActivationFunctionType
+
+P = 128
+PACK = 4
+BANK = 512
+HALF = SLOTS // 2
+LIST_COLS = SLOTS // 16
+
+
+def tile_attend_gatedpage_three_kernel(tc, query, cache_words, cache_scales, draft_words, draft_scales,
+                                        arch_words, arch_scales, offs, offs2, offs3, offs4, offs5, offs6, out):
+    nc = tc.nc
+    with ExitStack() as ctx:
+        keep = ctx.enter_context(tc.tile_pool(name="keep", bufs=1))
+        psum = ctx.enter_context(tc.psum_pool(name="psum", bufs=1))
+
+        def sbuf(name, shape, dtype):
+            return keep.tile(shape, dtype, name=name, align_bytes=64)
+
+        def load_list(name, src):
+            tile = keep.tile([P, LIST_COLS], U16, name=name)
+            nc.sync.dma_start(tile[:], src)
+            return tile
+
+        def load_scales(queue, plane, src):
+            for quad in range(4):
+                queue.dma_start(plane[32 * quad : 32 * quad + 4, :].bitcast(I32),
+                                src[0, 4 * quad : 4 * quad + 4, :].bitcast(I32))
+
+        def half(lst, h):
+            return lst[:, h * LIST_COLS // 2 : (h + 1) * LIST_COLS // 2]
+
+        def cols(h, width):
+            return slice(h * width, (h + 1) * width)
+
+        draft_plane = sbuf("draft_plane", [P, T], U8)
+        cache_plane = sbuf("cache_plane", [P, T], U8)
+        arch_plane = sbuf("arch_plane", [P, T], U8)
+        f1 = sbuf("f1", [P, T], F32)
+        f2 = sbuf("f2", [P, T], F32)
+        nc.vector.memset(draft_plane[:].bitcast(I32), 0)
+        nc.gpsimd.memset(cache_plane[:].bitcast(I32), 0)
+        nc.gpsimd.memset(arch_plane[:].bitcast(I32), 0)
+        nc.vector.memset(f1[:], 0.0)
+        nc.vector.memset(f2[:], 0.0)
+
+        q_raw = sbuf("q_raw", [P, PACK, Q], F32)
+        nc.sync.dma_start(q_raw[:], query.rearrange("(p j) q -> p j q", j=PACK))
+        draft_codes = sbuf("draft_codes", [P, 2 * T], U8)
+        nc.sync.dma_start(draft_codes[:].bitcast(I32), draft_words[0].bitcast(I32))
+        load_scales(nc.scalar, draft_plane, draft_scales)
+        list1 = load_list("list1", offs)
+        list2 = load_list("list2", offs2)
+        list4 = load_list("list4", offs4)
+        cache_codes = sbuf("cache_codes", [P, T], I32)
+        nc.sync.dma_start(cache_codes[:], cache_words[0].rearrange("p n t -> p (n t)").bitcast(I32))
+        load_scales(nc.sync, cache_plane, cache_scales)
+        list3 = load_list("list3", offs3)
+        list5 = load_list("list5", offs5)
+        arch_codes = sbuf("arch_codes", [P, T], I32)
+        nc.sync.dma_start(arch_codes[:], arch_words[0].rearrange("p n t -> p (n t)").bitcast(I32))
+        load_scales(nc.sync, arch_plane, arch_scales)
+        list6 = load_list("list6", offs6)
+
+        q_grouped = sbuf("q_grouped", [P, Q, PACK], BF16)
+        nc.vector.tensor_copy(out=q_grouped[:].rearrange("p (c i) j -> p c j i", i=4),
+                              in_=q_raw[:].rearrange("p j (c i) -> p c j i", i=4))
+        q_codes = sbuf("q_codes", [P, Q], U32)
+        q_plane = sbuf("q_plane", [P, Q], U8)
+        nc.vector.quantize_mx(out=q_codes[:].bitcast(FP8X4), scales=q_plane[:],
+                              in_=q_grouped[:].rearrange("p q j -> p (q j)"))
+
+        def score(name, rhs, rhs_scale, width):
+            acc = psum.tile([P, width], F32, name=name)
+            nc.tensor.matmul_mx(out=acc[:], lhsT=q_codes[:].bitcast(FP8X4), lhsT_scale=q_plane[:],
+                                rhs=rhs, rhs_scale=rhs_scale, start=True, stop=True)
+            return acc
+
+        b = sbuf("b", [P, T], F32)
+        piece = T // 4
+        for n in range(4):
+            acc = score("b_acc%d" % n, draft_codes[:, cols(n, 2 * piece)].bitcast(FP4X4),
+                        draft_plane[:, cols(n, piece)], piece)
+            if n % 2 == 0:
+                nc.scalar.activation(b[:, cols(n, piece)], acc[:], ACT.Copy)
+            else:
+                nc.vector.tensor_copy(b[:, cols(n, piece)], acc[:])
+        a_acc = [score("a_acc%d" % n, cache_codes[:, cols(n, BANK)].bitcast(FP8X4), cache_plane[:, cols(n, BANK)], BANK)
+                 for n in range(2)]
+        c_acc = [score("c_acc%d" % n, arch_codes[:, cols(n, BANK)].bitcast(FP8X4), arch_plane[:, cols(n, BANK)], BANK)
+                 for n in range(2)]
+
+        for h in range(2):
+            picked = sbuf("picked%d" % h, [P, HALF], F32)
+            nc.vector.tensor_copy(picked[:], b[:].indirect(half(list1, h)))
+            nc.scalar.activation(f1[:].indirect(half(list2, h)), picked[:], ACT.Copy)
+
+        b4 = sbuf("b4", [P, SLOTS], F32)
+        nc.vector.tensor_copy(b4[:], b[:].indirect(list4[:]))
+        a_half = sbuf("a_half", [P, T], F32)
+        for n in range(2):
+            nc.vector.tensor_scalar(a_half[:, cols(n, BANK)], a_acc[n][:], 0.5, None, ALU.mult)
+
+        th = sbuf("th", [P, T], F32)
+        mg = sbuf("mg", [P, T], F32)
+        for n in range(4):
+            nc.scalar.activation(th[:, cols(n, piece)], f1[:, cols(n, piece)], ACT.Tanh)
+            nc.vector.scalar_tensor_tensor(mg[:, cols(n, piece)], th[:, cols(n, piece)], 1.0,
+                                           a_half[:, cols(n, piece)], ALU.add, ALU.mult)
+
+        m3 = []
+        for h in range(2):
+            m3.append(sbuf("m3_%d" % h, [P, HALF], F32))
+            w = sbuf("w%d" % h, [P, HALF], F32)
+            nc.vector.tensor_copy(m3[h][:], mg[:].indirect(half(list3, h)))
+            nc.vector.tensor_tensor(w[:], m3[h][:], b4[:, cols(h, HALF)], ALU.max)
+            nc.scalar.activation(f2[:].indirect(half(list5, h)), w[:], ACT.Copy)
+
+        cc = sbuf("cc", [P, T], F32)
+        for n in range(2):
+            nc.vector.tensor_tensor(cc[:, cols(n, BANK)], c_acc[n][:], f2[:, cols(n, BANK)], ALU.subtract)
+
+        for h in range(2):
+            y = sbuf("y%d" % h, [P, HALF], F32)
+            nc.vector.tensor_tensor(y[:], cc[:].indirect(half(list6, h)), m3[h][:], ALU.add)
+            nc.sync.dma_start(out[:, cols(h, HALF)], y[:])

@@ -20,6 +20,8 @@ P = 128
 PACK = 4
 BANK = 512
 HALF = SLOTS // 2
+GATE = 128
+FIRST = 128
 LIST_COLS = SLOTS // 16
 
 
@@ -30,8 +32,8 @@ def tile_attend_gatedpage_three_kernel(tc, query, cache_words, cache_scales, dra
         keep = ctx.enter_context(tc.tile_pool(name="keep", bufs=1))
         psum = ctx.enter_context(tc.psum_pool(name="psum", bufs=1))
 
-        def sbuf(name, shape, dtype):
-            return keep.tile(shape, dtype, name=name, align_bytes=64)
+        def sbuf(name, shape, dtype, tag=None):
+            return keep.tile(shape, dtype, name=name, tag=tag or name, align_bytes=64)
 
         def load_list(name, src):
             tile = keep.tile([P, LIST_COLS], U16, name=name)
@@ -53,12 +55,10 @@ def tile_attend_gatedpage_three_kernel(tc, query, cache_words, cache_scales, dra
         cache_plane = sbuf("cache_plane", [P, T], U8)
         arch_plane = sbuf("arch_plane", [P, T], U8)
         f1 = sbuf("f1", [P, T], F32)
-        f2 = sbuf("f2", [P, T], F32)
-        nc.vector.memset(draft_plane[:].bitcast(I32), 0)
+        nc.gpsimd.memset(draft_plane[:].bitcast(I32), 0)
         nc.gpsimd.memset(cache_plane[:].bitcast(I32), 0)
         nc.gpsimd.memset(arch_plane[:].bitcast(I32), 0)
         nc.vector.memset(f1[:], 0.0)
-        nc.vector.memset(f2[:], 0.0)
 
         q_raw = sbuf("q_raw", [P, PACK, Q], F32)
         nc.sync.dma_start(q_raw[:], query.rearrange("(p j) q -> p j q", j=PACK))
@@ -93,23 +93,21 @@ def tile_attend_gatedpage_three_kernel(tc, query, cache_words, cache_scales, dra
             return acc
 
         b = sbuf("b", [P, T], F32)
-        piece = T // 4
-        for n in range(4):
-            acc = score("b_acc%d" % n, draft_codes[:, cols(n, 2 * piece)].bitcast(FP4X4),
-                        draft_plane[:, cols(n, piece)], piece)
-            if n % 2 == 0:
-                nc.scalar.activation(b[:, cols(n, piece)], acc[:], ACT.Copy)
+        for lo, hi, on_vector in ((0, 512, True), (512, 768, False), (768, 896, False), (896, T, True)):
+            acc = score("b_acc%d" % lo, draft_codes[:, 2 * lo : 2 * hi].bitcast(FP4X4), draft_plane[:, lo:hi], hi - lo)
+            if on_vector:
+                nc.vector.tensor_copy(b[:, lo:hi], acc[:])
             else:
-                nc.vector.tensor_copy(b[:, cols(n, piece)], acc[:])
+                nc.scalar.activation(b[:, lo:hi], acc[:], ACT.Copy)
         a_acc = [score("a_acc%d" % n, cache_codes[:, cols(n, BANK)].bitcast(FP8X4), cache_plane[:, cols(n, BANK)], BANK)
                  for n in range(2)]
         c_acc = [score("c_acc%d" % n, arch_codes[:, cols(n, BANK)].bitcast(FP8X4), arch_plane[:, cols(n, BANK)], BANK)
                  for n in range(2)]
 
-        for h in range(2):
-            picked = sbuf("picked%d" % h, [P, HALF], F32)
-            nc.vector.tensor_copy(picked[:], b[:].indirect(half(list1, h)))
-            nc.scalar.activation(f1[:].indirect(half(list2, h)), picked[:], ACT.Copy)
+        picked = sbuf("picked", [P, SLOTS], F32)
+        nc.vector.tensor_copy(picked[:, cols(0, HALF)], b[:].indirect(half(list1, 0)))
+        nc.scalar.activation(picked[:, cols(1, HALF)], b[:].indirect(half(list1, 1)), ACT.Copy)
+        nc.scalar.activation(f1[:].indirect(list2[:]), picked[:], ACT.Copy)
 
         b4 = sbuf("b4", [P, SLOTS], F32)
         nc.vector.tensor_copy(b4[:], b[:].indirect(list4[:]))
@@ -117,26 +115,36 @@ def tile_attend_gatedpage_three_kernel(tc, query, cache_words, cache_scales, dra
         for n in range(2):
             nc.vector.tensor_scalar(a_half[:, cols(n, BANK)], a_acc[n][:], 0.5, None, ALU.mult)
 
+        f2_first = sbuf("f2_first", [P, T], F32, tag="b")
+        nc.vector.memset(f2_first[:], 0.0)
+        f2_rest = sbuf("f2_rest", [P, T], F32, tag="cache_codes")
+        nc.gpsimd.memset(f2_rest[:], 0.0)
+
         th = sbuf("th", [P, T], F32)
         mg = sbuf("mg", [P, T], F32)
-        for n in range(4):
-            nc.scalar.activation(th[:, cols(n, piece)], f1[:, cols(n, piece)], ACT.Tanh)
-            nc.vector.scalar_tensor_tensor(mg[:, cols(n, piece)], th[:, cols(n, piece)], 1.0,
-                                           a_half[:, cols(n, piece)], ALU.add, ALU.mult)
+        for n in range(T // GATE):
+            nc.scalar.activation(th[:, cols(n, GATE)], f1[:, cols(n, GATE)], ACT.Tanh)
+            nc.vector.scalar_tensor_tensor(mg[:, cols(n, GATE)], th[:, cols(n, GATE)], 1.0,
+                                           a_half[:, cols(n, GATE)], ALU.add, ALU.mult)
 
-        m3 = []
-        for h in range(2):
-            m3.append(sbuf("m3_%d" % h, [P, HALF], F32))
-            w = sbuf("w%d" % h, [P, HALF], F32)
-            nc.vector.tensor_copy(m3[h][:], mg[:].indirect(half(list3, h)))
-            nc.vector.tensor_tensor(w[:], m3[h][:], b4[:, cols(h, HALF)], ALU.max)
-            nc.scalar.activation(f2[:].indirect(half(list5, h)), w[:], ACT.Copy)
+        m3 = sbuf("m3", [P, SLOTS], F32)
+        nc.vector.tensor_copy(m3[:, cols(0, HALF)], mg[:].indirect(half(list3, 0)))
+        nc.scalar.activation(m3[:, cols(1, HALF)], mg[:].indirect(half(list3, 1)), ACT.Copy)
+        w = sbuf("w", [P, SLOTS], F32)
+        for f2, lo, hi in ((f2_first, 0, FIRST), (f2_rest, FIRST, SLOTS)):
+            nc.vector.tensor_tensor(w[:, lo:hi], m3[:, lo:hi], b4[:, lo:hi], ALU.max)
+            nc.scalar.activation(f2[:].indirect(list5[:, lo // 16 : hi // 16]), w[:, lo:hi], ACT.Copy)
 
         cc = sbuf("cc", [P, T], F32)
+        c_less = sbuf("c_less", [P, T], F32)
         for n in range(2):
-            nc.vector.tensor_tensor(cc[:, cols(n, BANK)], c_acc[n][:], f2[:, cols(n, BANK)], ALU.subtract)
+            nc.vector.tensor_tensor(c_less[:, cols(n, BANK)], c_acc[n][:], f2_first[:, cols(n, BANK)], ALU.subtract)
+        nc.vector.tensor_tensor(cc[:], c_less[:], f2_rest[:], ALU.subtract)
 
-        for h in range(2):
-            y = sbuf("y%d" % h, [P, HALF], F32)
-            nc.vector.tensor_tensor(y[:], cc[:].indirect(half(list6, h)), m3[h][:], ALU.add)
-            nc.sync.dma_start(out[:, cols(h, HALF)], y[:])
+        y = sbuf("y", [P, SLOTS], F32)
+        c6 = sbuf("c6", [P, HALF], F32)
+        nc.scalar.activation(c6[:], cc[:].indirect(half(list6, 1)), ACT.Copy)
+        nc.vector.tensor_tensor(y[:, cols(0, HALF)], cc[:].indirect(half(list6, 0)), m3[:, cols(0, HALF)], ALU.add)
+        nc.sync.dma_start(out[:, cols(0, HALF)], y[:, cols(0, HALF)])
+        nc.vector.tensor_tensor(y[:, cols(1, HALF)], c6[:], m3[:, cols(1, HALF)], ALU.add)
+        nc.sync.dma_start(out[:, cols(1, HALF)], y[:, cols(1, HALF)])

from contextlib import ExitStack

import concourse.mybir as mybir

D, T, SLOTS, Q = 512, 1024, 512, 128
FLOPS = 3 * 2 * D * T * Q

F32 = mybir.dt.float32
BF16 = mybir.dt.bfloat16
I32 = mybir.dt.int32
U32 = mybir.dt.uint32
U16 = mybir.dt.uint16
U8 = mybir.dt.uint8
FP8X4 = mybir.dt.float8_e4m3fn_x4
FP4X4 = mybir.dt.float4_e2m1fn_x4
ALU = mybir.AluOpType
ACT = mybir.ActivationFunctionType

P = 128
PACK = 4
BANK = 512
HALF = SLOTS // 2
GATE = 128
FIRST = 128
LIST_COLS = SLOTS // 16


def tile_attend_gatedpage_three_kernel(tc, query, cache_words, cache_scales, draft_words, draft_scales,
                                        arch_words, arch_scales, offs, offs2, offs3, offs4, offs5, offs6, out):
    nc = tc.nc
    with ExitStack() as ctx:
        keep = ctx.enter_context(tc.tile_pool(name="keep", bufs=1))
        psum = ctx.enter_context(tc.psum_pool(name="psum", bufs=1))

        def sbuf(name, shape, dtype, tag=None):
            return keep.tile(shape, dtype, name=name, tag=tag or name, align_bytes=64)

        def load_list(name, src):
            tile = keep.tile([P, LIST_COLS], U16, name=name)
            nc.sync.dma_start(tile[:], src)
            return tile

        def load_scales(queue, plane, src):
            for quad in range(4):
                queue.dma_start(plane[32 * quad : 32 * quad + 4, :].bitcast(I32),
                                src[0, 4 * quad : 4 * quad + 4, :].bitcast(I32))

        def half(lst, h):
            return lst[:, h * LIST_COLS // 2 : (h + 1) * LIST_COLS // 2]

        def cols(h, width):
            return slice(h * width, (h + 1) * width)

        draft_plane = sbuf("draft_plane", [P, T], U8)
        cache_plane = sbuf("cache_plane", [P, T], U8)
        arch_plane = sbuf("arch_plane", [P, T], U8)
        f1 = sbuf("f1", [P, T], F32)
        nc.gpsimd.memset(draft_plane[:].bitcast(I32), 0)
        nc.gpsimd.memset(cache_plane[:].bitcast(I32), 0)
        nc.gpsimd.memset(arch_plane[:].bitcast(I32), 0)
        nc.vector.memset(f1[:], 0.0)

        q_raw = sbuf("q_raw", [P, PACK, Q], F32)
        nc.sync.dma_start(q_raw[:], query.rearrange("(p j) q -> p j q", j=PACK))
        draft_codes = sbuf("draft_codes", [P, 2 * T], U8)
        nc.sync.dma_start(draft_codes[:].bitcast(I32), draft_words[0].bitcast(I32))
        load_scales(nc.scalar, draft_plane, draft_scales)
        list1 = load_list("list1", offs)
        list2 = load_list("list2", offs2)
        list4 = load_list("list4", offs4)
        cache_codes = sbuf("cache_codes", [P, T], I32)
        nc.sync.dma_start(cache_codes[:], cache_words[0].rearrange("p n t -> p (n t)").bitcast(I32))
        load_scales(nc.sync, cache_plane, cache_scales)
        list3 = load_list("list3", offs3)
        list5 = load_list("list5", offs5)
        arch_codes = sbuf("arch_codes", [P, T], I32)
        nc.sync.dma_start(arch_codes[:], arch_words[0].rearrange("p n t -> p (n t)").bitcast(I32))
        load_scales(nc.sync, arch_plane, arch_scales)
        list6 = load_list("list6", offs6)

        q_grouped = sbuf("q_grouped", [P, Q, PACK], BF16)
        nc.vector.tensor_copy(out=q_grouped[:].rearrange("p (c i) j -> p c j i", i=4),
                              in_=q_raw[:].rearrange("p j (c i) -> p c j i", i=4))
        q_codes = sbuf("q_codes", [P, Q], U32)
        q_plane = sbuf("q_plane", [P, Q], U8)
        nc.vector.quantize_mx(out=q_codes[:].bitcast(FP8X4), scales=q_plane[:],
                              in_=q_grouped[:].rearrange("p q j -> p (q j)"))

        def score(name, rhs, rhs_scale, width):
            acc = psum.tile([P, width], F32, name=name)
            nc.tensor.matmul_mx(out=acc[:], lhsT=q_codes[:].bitcast(FP8X4), lhsT_scale=q_plane[:],
                                rhs=rhs, rhs_scale=rhs_scale, start=True, stop=True)
            return acc

        b = sbuf("b", [P, T], F32)
        for lo, hi, on_vector in ((0, 512, True), (512, 768, False), (768, 896, False), (896, T, True)):
            acc = score("b_acc%d" % lo, draft_codes[:, 2 * lo : 2 * hi].bitcast(FP4X4), draft_plane[:, lo:hi], hi - lo)
            if on_vector:
                nc.vector.tensor_copy(b[:, lo:hi], acc[:])
            else:
                nc.scalar.activation(b[:, lo:hi], acc[:], ACT.Copy)
        a_acc = [score("a_acc%d" % n, cache_codes[:, cols(n, BANK)].bitcast(FP8X4), cache_plane[:, cols(n, BANK)], BANK)
                 for n in range(2)]
        c_acc = [score("c_acc%d" % n, arch_codes[:, cols(n, BANK)].bitcast(FP8X4), arch_plane[:, cols(n, BANK)], BANK)
                 for n in range(2)]

        picked = sbuf("picked", [P, SLOTS], F32)
        nc.vector.tensor_copy(picked[:, cols(0, HALF)], b[:].indirect(half(list1, 0)))
        nc.scalar.activation(picked[:, cols(1, HALF)], b[:].indirect(half(list1, 1)), ACT.Copy)
        nc.scalar.activation(f1[:].indirect(list2[:]), picked[:], ACT.Copy)

        b4 = sbuf("b4", [P, SLOTS], F32)
        nc.vector.tensor_copy(b4[:], b[:].indirect(list4[:]))
        a_half = sbuf("a_half", [P, T], F32)
        for n in range(2):
            nc.vector.tensor_scalar(a_half[:, cols(n, BANK)], a_acc[n][:], 0.5, None, ALU.mult)

        f2_first = sbuf("f2_first", [P, T], F32, tag="b")
        nc.vector.memset(f2_first[:], 0.0)
        f2_rest = sbuf("f2_rest", [P, T], F32, tag="cache_codes")
        nc.gpsimd.memset(f2_rest[:], 0.0)

        th = sbuf("th", [P, T], F32)
        mg = sbuf("mg", [P, T], F32)
        for n in range(T // GATE):
            nc.scalar.activation(th[:, cols(n, GATE)], f1[:, cols(n, GATE)], ACT.Tanh)
            nc.vector.scalar_tensor_tensor(mg[:, cols(n, GATE)], th[:, cols(n, GATE)], 1.0,
                                           a_half[:, cols(n, GATE)], ALU.add, ALU.mult)

        m3 = sbuf("m3", [P, SLOTS], F32)
        nc.vector.tensor_copy(m3[:, cols(0, HALF)], mg[:].indirect(half(list3, 0)))
        nc.scalar.activation(m3[:, cols(1, HALF)], mg[:].indirect(half(list3, 1)), ACT.Copy)
        w = sbuf("w", [P, SLOTS], F32)
        for f2, lo, hi in ((f2_first, 0, FIRST), (f2_rest, FIRST, SLOTS)):
            nc.vector.tensor_tensor(w[:, lo:hi], m3[:, lo:hi], b4[:, lo:hi], ALU.max)
            nc.scalar.activation(f2[:].indirect(list5[:, lo // 16 : hi // 16]), w[:, lo:hi], ACT.Copy)

        cc = sbuf("cc", [P, T], F32)
        c_less = sbuf("c_less", [P, T], F32)
        for n in range(2):
            nc.vector.tensor_tensor(c_less[:, cols(n, BANK)], c_acc[n][:], f2_first[:, cols(n, BANK)], ALU.subtract)
        nc.vector.tensor_tensor(cc[:], c_less[:], f2_rest[:], ALU.subtract)

        y = sbuf("y", [P, SLOTS], F32)
        c6 = sbuf("c6", [P, HALF], F32)
        nc.scalar.activation(c6[:], cc[:].indirect(half(list6, 1)), ACT.Copy)
        nc.vector.tensor_tensor(y[:, cols(0, HALF)], cc[:].indirect(half(list6, 0)), m3[:, cols(0, HALF)], ALU.add)
        nc.sync.dma_start(out[:, cols(0, HALF)], y[:, cols(0, HALF)])
        nc.vector.tensor_tensor(y[:, cols(1, HALF)], c6[:], m3[:, cols(1, HALF)], ALU.add)
        nc.sync.dma_start(out[:, cols(1, HALF)], y[:, cols(1, HALF)])
